import numpy as np
import ml_dtypes


def mxq(x, axis, fmt="e4m3"):
    dtype, down = {"e4m3": (ml_dtypes.float8_e4m3fn, 7), "e5m2": (ml_dtypes.float8_e5m2, 14)}[fmt]
    v = np.moveaxis(np.asarray(x, np.float32).astype(ml_dtypes.bfloat16).astype(np.float64), axis, -1)
    blocks = v.reshape(v.shape[:-1] + (-1, 32))
    amax = np.abs(blocks).max(-1, keepdims=True)
    byte = np.maximum(np.where(amax > 0, np.frexp(amax)[1] - 1 + 127, 0) - down, 1)
    scale = np.exp2(byte - 127.0)
    codes = (blocks / scale).astype(np.float32).astype(dtype).astype(np.float64)
    return np.moveaxis((codes * scale).reshape(v.shape), -1, axis)


WIDE = False


def mx_kscale(k):
    if not WIDE:
        return np.ones(k)
    levels = np.array([10, -10, 5, -5, 0])
    if k % 512:
        return np.exp2(np.random.permutation(np.resize(levels, k // 32))).repeat(32)
    a = np.empty((k // 512, 16))
    for p in range(k // 512):
        a[p, :8] = np.random.permutation(np.resize(levels, 8))
        for g in range(8):
            far = levels[np.abs(levels - a[p, g]) >= 10]
            a[p, g + 8] = far[np.random.randint(len(far))]
    return np.exp2(a.ravel()).repeat(32)


def f64(x):
    return np.asarray(x).astype(np.float64)


def striped8(idx):
    return np.asarray(idx).reshape(8, -1, 16).transpose(0, 2, 1).reshape(128, -1).astype(np.uint16)


def unstriped8(offs):
    return offs.reshape(8, 16, -1).transpose(0, 2, 1).reshape(8, -1).astype(np.int64)


def pick8(x, idx, run):
    r = np.arange(len(x))
    return x[r[:, None], idx[r % (8 * run) // run]]


E2M1 = np.array([0.0, 0.5, 1.0, 1.5, 2.0, 3.0, 4.0, 6.0, -0.0, -0.5, -1.0, -1.5, -2.0, -3.0, -4.0, -6.0])


def pack_weight(w, fmt):
    k, n = w.shape
    w = f64(np.asarray(w, np.float32).astype(ml_dtypes.bfloat16)).reshape(k // 32, 32, n)
    amax = np.abs(w).max(1)
    if fmt == "e4m3":
        byte = np.frexp(amax)[1] - 1 + 127 - 7
    else:
        mant, ex = np.frexp(amax / 6.0)
        byte = np.where(mant > 0.5, ex, ex - 1) + 127
    byte = np.clip(np.where(amax > 0, byte, 1), 1, 254)
    scaled = (w * np.exp2(127.0 - byte)[:, None, :]).reshape(k, n).astype(np.float32)
    by_word = np.ascontiguousarray(scaled.reshape(k // 512, 128, 4, n).transpose(0, 1, 3, 2))
    if fmt == "e4m3":
        words = by_word.astype(ml_dtypes.float8_e4m3fn).view(np.uint8)
    else:
        c = by_word.astype(ml_dtypes.float4_e2m1fn).view(np.uint8) & 0xF
        words = (c[..., 0::2] | (c[..., 1::2] << 4)).reshape(k // 512, 128, 2 * n)
    return np.ascontiguousarray(words), np.ascontiguousarray(byte.astype(np.uint8).reshape(k // 512, 16, n))


def unpack_weight(words, scales, fmt):
    g, _, n = scales.shape
    words = np.ascontiguousarray(words).reshape(g, 128, n, -1)
    if fmt == "e4m3":
        vals = words.view(ml_dtypes.float8_e4m3fn).astype(np.float64)
    else:
        nib = np.empty((g, 128, n, 4), np.uint8)
        nib[..., 0::2] = words & 0xF
        nib[..., 1::2] = words >> 4
        vals = E2M1[nib]
    vals = vals * np.repeat(np.exp2(scales.astype(np.float64) - 127.0), 8, axis=1)[..., None]
    return vals.transpose(0, 1, 3, 2).reshape(g * 512, n)


D, T, I, Q = 512, 1024, 512, 128


def setup_inputs():
    n = np.random.standard_normal
    idx = np.stack([np.random.permutation(T)[:I] for _ in range(8)])
    idx2 = np.stack([np.random.permutation(T)[:I] for _ in range(8)])
    idx3 = np.stack([np.random.permutation(T)[:I] for _ in range(8)])
    fd = mx_kscale(D)
    keysp = pack_weight(n((D, T)) / fd[:, None], "e4m3")
    return {
        "query": (n((D, Q)) * 1.0 / np.sqrt(D) * fd[:, None]).astype(np.float32),
        "keys_words": keysp[0],
        "keys_scales": keysp[1],
        "old": (1.0 * n((Q, T))).astype(np.float32),
        "offs": striped8(idx),
        "offs2": striped8(idx2),
        "offs3": striped8(idx3),
    }


def reference(query, keys_words, keys_scales, old, offs, offs2, offs3):
    idx = unstriped8(offs)
    idx2 = unstriped8(offs2)
    idx3 = unstriped8(offs3)
    keysu = unpack_weight(keys_words, keys_scales, "e4m3")
    queryq = mxq(f64(query), 0, "e4m3")
    a = queryq.T @ keysu
    w = pick8(a, idx, 16) - pick8(a, idx2, 16)
    f1 = np.zeros((Q, T))
    f1[np.arange(Q)[:, None], idx3[np.arange(Q) % 128 // 16]] = w
    y = np.maximum(f1, f64(old)) + f64(old) * 0.25
    return y

@@ -1,0 +1,127 @@
+from contextlib import ExitStack
+
+import concourse.mybir as mybir
+
+D, T, I, Q = 512, 1024, 512, 128
+FLOPS = 2 * D * T * Q
+
+F32 = mybir.dt.float32
+BF16 = mybir.dt.bfloat16
+U32 = mybir.dt.uint32
+I32 = mybir.dt.int32
+U16 = mybir.dt.uint16
+U8 = mybir.dt.uint8
+FP8X4 = mybir.dt.float8_e4m3fn_x4
+ALU = mybir.AluOpType
+COPY = mybir.ActivationFunctionType.Copy
+
+P = 128
+PACK = 4
+GROUP = 16
+MM_WIDTHS = (256, 256, 256, 128, 128)
+HALF = I // 2
+N_OUT = 256
+
+
+def tile_attend_difference_lean_largerput_heads_kernel(
+    tc, query, keys_words, keys_scales, old, offs, offs2, offs3, out
+):
+    nc = tc.nc
+    with ExitStack() as ctx:
+        keep = ctx.enter_context(tc.tile_pool(name="keep", bufs=1))
+        psum = ctx.enter_context(tc.psum_pool(name="psum", bufs=1))
+
+        list1 = keep.tile([P, I // GROUP], U16, name="list1")
+        list2 = keep.tile([P, I // GROUP], U16, name="list2")
+        list3 = keep.tile([P, I // GROUP], U16, name="list3")
+        q_raw = keep.tile([P, PACK, Q], F32, name="q_raw")
+        k_words = keep.tile([P, T], U32, name="k_words", align_bytes=64)
+        k_scales = keep.tile([P, T], U8, name="k_scales", align_bytes=64)
+        old_sb = keep.tile([P, T], F32, name="old_sb")
+        placed = keep.tile([P, T], F32, name="placed")
+        scores = keep.tile([P, T], F32, name="scores")
+
+        nc.vector.memset(k_scales[:].bitcast(I32), 0)
+        nc.sync.dma_start(out=q_raw[:], in_=query.rearrange("(p j) q -> p j q", j=PACK))
+        for quad in range(4):
+            nc.scalar.dma_start(
+                out=k_scales[32 * quad : 32 * quad + 4, :].bitcast(I32),
+                in_=keys_scales[0, 4 * quad : 4 * quad + 4, :].bitcast(I32),
+            )
+        nc.sync.dma_start(
+            out=k_words[:].bitcast(I32),
+            in_=keys_words[0].rearrange("p t r -> p (t r)").bitcast(I32),
+        )
+        nc.sync.dma_start(list1[:], offs)
+        nc.sync.dma_start(list2[:], offs2)
+        nc.sync.dma_start(list3[:], offs3)
+        nc.sync.dma_start(out=old_sb[:], in_=old)
+        nc.vector.memset(placed[:], 0.0)
+
+        q_bf = keep.tile([P, Q, PACK], BF16, name="q_bf", align_bytes=64)
+        q_words = keep.tile([P, Q], U32, name="q_words", align_bytes=64)
+        q_scales = keep.tile([P, Q], U8, name="q_scales", align_bytes=64)
+        halves = [slice(0, Q // 2), slice(Q // 2, Q)]
+        for rows in halves:
+            nc.vector.tensor_copy(
+                out=q_bf[:, rows, :].rearrange("p (c i) j -> p c j i", i=4),
+                in_=q_raw[:, :, rows].rearrange("p j (c i) -> p c j i", i=4),
+            )
+        for rows in halves:
+            nc.vector.quantize_mx(
+                out=q_words[:, rows].bitcast(FP8X4),
+                scales=q_scales[:, rows],
+                in_=q_bf[:, rows, :].rearrange("p q j -> p (q j)"),
+            )
+
+        for c, width in enumerate(MM_WIDTHS):
+            first = sum(MM_WIDTHS[:c])
+            cols = slice(first, first + width)
+            bank = psum.tile([P, width], F32, name="bank%d" % c)
+            nc.tensor.matmul_mx(
+                out=bank[:],
+                lhsT=q_words[:].bitcast(FP8X4),
+                lhsT_scale=q_scales[:],
+                rhs=k_words[:, cols].bitcast(FP8X4),
+                rhs_scale=k_scales[:, cols],
+                start=True,
+                stop=True,
+            )
+            if c % 2 == 0:
+                nc.scalar.copy(out=scores[:, cols], in_=bank[:])
+            else:
+                nc.vector.tensor_copy(out=scores[:, cols], in_=bank[:])
+
+        for h in range(2):
+            part = slice(h * HALF // GROUP, (h + 1) * HALF // GROUP)
+            plus = keep.tile([P, HALF], F32, name="plus%d" % h)
+            minus = keep.tile([P, HALF], F32, name="minus%d" % h)
+            nc.scalar.activation(plus[:], scores[:].indirect(list1[:, part]), COPY)
+            if h == 0:
+                nc.vector.tensor_scalar(
+                    minus[:], scores[:].indirect(list2[:, part]), -1.0, 0.0, ALU.mult, ALU.add
+                )
+            else:
+                nc.scalar.activation(
+                    minus[:], scores[:].indirect(list2[:, part]), COPY, scale=-1.0
+                )
+            nc.vector.tensor_tensor(
+                placed[:].indirect(list3[:, part]), plus[:], minus[:], ALU.add
+            )
+
+        chunks = [slice(c * N_OUT, (c + 1) * N_OUT) for c in range(T // N_OUT)]
+        larger = [keep.tile([P, N_OUT], F32, name="larger%d" % c) for c in range(len(chunks))]
+        result = [keep.tile([P, N_OUT], F32, name="result%d" % c) for c in range(len(chunks))]
+        for step in range(len(chunks) + 1):
+            if step < len(chunks):
+                cols = chunks[step]
+                nc.vector.tensor_tensor(
+                    larger[step][:], placed[:, cols], old_sb[:, cols], ALU.max
+                )
+            if step > 0:
+                c = step - 1
+                nc.vector.scalar_tensor_tensor(
+                    result[c][:], old_sb[:, chunks[c]], 0.25, larger[c][:], ALU.mult, ALU.add
+                )
+                queue = nc.sync if c % 2 == 0 else nc.scalar
+                queue.dma_start(out=out[:, chunks[c]], in_=result[c][:])

@@ -1,6 +1,7 @@
 from contextlib import ExitStack
 
 import concourse.mybir as mybir
+from concourse.masks import make_identity
 
 D, T, I, Q = 512, 1024, 512, 128
 FLOPS = 2 * D * T * Q
@@ -21,6 +22,7 @@ GROUP = 16
 MM_WIDTHS = (256, 256, 256, 128, 128)
 HALF = I // 2
 N_OUT = 256
+BANK = 512
 
 
 def tile_attend_difference_lean_largerput_heads_kernel(
@@ -35,7 +37,10 @@ def tile_attend_difference_lean_largerput_heads_kernel(
         list2 = keep.tile([P, I // GROUP], U16, name="list2")
         list3 = keep.tile([P, I // GROUP], U16, name="list3")
         q_raw = keep.tile([P, PACK, Q], F32, name="q_raw")
-        k_words = keep.tile([P, T], U32, name="k_words", align_bytes=64)
+        k_words = [
+            keep.tile([P, BANK], U32, name="k_words%d" % b, align_bytes=64) for b in range(2)
+        ]
+        ident = keep.tile([P, P], F32, name="ident")
         k_scales = keep.tile([P, T], U8, name="k_scales", align_bytes=64)
         old_sb = keep.tile([P, T], F32, name="old_sb")
         placed = keep.tile([P, T], F32, name="placed")
@@ -43,20 +48,28 @@ def tile_attend_difference_lean_largerput_heads_kernel(
 
         nc.vector.memset(k_scales[:].bitcast(I32), 0)
         nc.sync.dma_start(out=q_raw[:], in_=query.rearrange("(p j) q -> p j q", j=PACK))
+
+        def load_words(b):
+            nc.sync.dma_start(
+                out=k_words[b][:].bitcast(I32),
+                in_=keys_words[0, :, b * BANK : (b + 1) * BANK, :]
+                .rearrange("p t r -> p (t r)")
+                .bitcast(I32),
+            )
+
+        load_words(0)
         for quad in range(4):
-            nc.scalar.dma_start(
+            nc.sync.dma_start(
                 out=k_scales[32 * quad : 32 * quad + 4, :].bitcast(I32),
                 in_=keys_scales[0, 4 * quad : 4 * quad + 4, :].bitcast(I32),
             )
-        nc.sync.dma_start(
-            out=k_words[:].bitcast(I32),
-            in_=keys_words[0].rearrange("p t r -> p (t r)").bitcast(I32),
-        )
+        load_words(1)
         nc.sync.dma_start(list1[:], offs)
         nc.sync.dma_start(list2[:], offs2)
         nc.sync.dma_start(list3[:], offs3)
         nc.sync.dma_start(out=old_sb[:], in_=old)
-        nc.vector.memset(placed[:], 0.0)
+        make_identity(nc, ident[:])
+        nc.gpsimd.memset(placed[:], 0.0)
 
         q_bf = keep.tile([P, Q, PACK], BF16, name="q_bf", align_bytes=64)
         q_words = keep.tile([P, Q], U32, name="q_words", align_bytes=64)
@@ -77,12 +90,12 @@ def tile_attend_difference_lean_largerput_heads_kernel(
         for c, width in enumerate(MM_WIDTHS):
             first = sum(MM_WIDTHS[:c])
             cols = slice(first, first + width)
-            bank = psum.tile([P, width], F32, name="bank%d" % c)
+            bank = psum.tile([P, width], F32, name="bank%d" % c, tag="bank%d" % c)
             nc.tensor.matmul_mx(
                 out=bank[:],
                 lhsT=q_words[:].bitcast(FP8X4),
                 lhsT_scale=q_scales[:],
-                rhs=k_words[:, cols].bitcast(FP8X4),
+                rhs=k_words[first // BANK][:, first % BANK : first % BANK + width].bitcast(FP8X4),
                 rhs_scale=k_scales[:, cols],
                 start=True,
                 stop=True,
@@ -109,19 +122,45 @@ def tile_attend_difference_lean_largerput_heads_kernel(
                 placed[:].indirect(list3[:, part]), plus[:], minus[:], ALU.add
             )
 
-        chunks = [slice(c * N_OUT, (c + 1) * N_OUT) for c in range(T // N_OUT)]
-        larger = [keep.tile([P, N_OUT], F32, name="larger%d" % c) for c in range(len(chunks))]
-        result = [keep.tile([P, N_OUT], F32, name="result%d" % c) for c in range(len(chunks))]
-        for step in range(len(chunks) + 1):
-            if step < len(chunks):
-                cols = chunks[step]
-                nc.vector.tensor_tensor(
-                    larger[step][:], placed[:, cols], old_sb[:, cols], ALU.max
+        old_ps = []
+        for b, factor in enumerate((1.0, 1.25)):
+            turned_ps = psum.tile([P, BANK], F32, name="turned_ps%d" % b, tag="bank%d" % b)
+            turned = keep.tile([P, BANK], F32, name="turned%d" % b)
+            back = psum.tile([P, BANK], F32, name="back%d" % b)
+            for s in range(BANK // P):
+                nc.tensor.transpose(
+                    turned_ps[:, s * P : (s + 1) * P],
+                    old_sb[:, b * BANK + s * P : b * BANK + (s + 1) * P],
+                    ident[:],
                 )
-            if step > 0:
-                c = step - 1
-                nc.vector.scalar_tensor_tensor(
-                    result[c][:], old_sb[:, chunks[c]], 0.25, larger[c][:], ALU.mult, ALU.add
+            nc.scalar.activation(turned[:], turned_ps[:], COPY, scale=factor)
+            for s in range(BANK // P):
+                nc.tensor.transpose(
+                    back[:, s * P : (s + 1) * P], turned[:, s * P : (s + 1) * P], ident[:]
                 )
-                queue = nc.sync if c % 2 == 0 else nc.scalar
-                queue.dma_start(out=out[:, chunks[c]], in_=result[c][:])
+            old_ps.append(back)
+
+        low = [slice(0, 256), slice(256, 512)]
+        high = [slice(0, 320), slice(320, 512)]
+        larger = [keep.tile([P, s.stop - s.start], F32, name="larger%d" % s.start) for s in low]
+        excess = [keep.tile([P, s.stop - s.start], F32, name="excess%d" % s.start) for s in high]
+        for c, part in enumerate(high):
+            cols = slice(BANK + part.start, BANK + part.stop)
+            nc.gpsimd.tensor_tensor(excess[c][:], placed[:, cols], old_sb[:, cols], ALU.subtract)
+        for c, part in enumerate(low):
+            nc.vector.tensor_tensor(larger[c][:], placed[:, part], old_ps[0][:, part], ALU.max)
+        for c, part in enumerate(low):
+            result = keep.tile([P, part.stop - part.start], F32, name="result_low%d" % c)
+            nc.vector.scalar_tensor_tensor(
+                result[:], old_ps[0][:, part], 0.25, larger[c][:], ALU.mult, ALU.add
+            )
+            queue = nc.sync if c % 2 == 0 else nc.scalar
+            queue.dma_start(out=out[:, part], in_=result[:])
+        for c, part in enumerate(high):
+            cols = slice(BANK + part.start, BANK + part.stop)
+            result = keep.tile([P, part.stop - part.start], F32, name="result_high%d" % c)
+            nc.vector.scalar_tensor_tensor(
+                result[:], excess[c][:], 0.0, old_ps[1][:, part], ALU.max, ALU.add
+            )
+            queue = nc.sync if c % 2 == 0 else nc.scalar
+            queue.dma_start(out=out[:, cols], in_=result[:])

@@ -40,7 +40,6 @@ def tile_attend_difference_lean_largerput_heads_kernel(
         k_words = [
             keep.tile([P, BANK], U32, name="k_words%d" % b, align_bytes=64) for b in range(2)
         ]
-        ident = keep.tile([P, P], F32, name="ident")
         k_scales = keep.tile([P, T], U8, name="k_scales", align_bytes=64)
         old_sb = keep.tile([P, T], F32, name="old_sb")
         placed = keep.tile([P, T], F32, name="placed")
@@ -68,10 +67,9 @@ def tile_attend_difference_lean_largerput_heads_kernel(
         nc.sync.dma_start(list2[:], offs2)
         nc.sync.dma_start(list3[:], offs3)
         nc.sync.dma_start(out=old_sb[:], in_=old)
-        make_identity(nc, ident[:])
-        nc.gpsimd.memset(placed[:], 0.0)
+        nc.vector.memset(placed[:], 0.0)
 
-        q_bf = keep.tile([P, Q, PACK], BF16, name="q_bf", align_bytes=64)
+        q_bf = keep.tile([P, Q, PACK], BF16, name="q_bf", tag="q_bf", align_bytes=64)
         q_words = keep.tile([P, Q], U32, name="q_words", align_bytes=64)
         q_scales = keep.tile([P, Q], U8, name="q_scales", align_bytes=64)
         halves = [slice(0, Q // 2), slice(Q // 2, Q)]
@@ -86,6 +84,9 @@ def tile_attend_difference_lean_largerput_heads_kernel(
                 scales=q_scales[:, rows],
                 in_=q_bf[:, rows, :].rearrange("p q j -> p (q j)"),
             )
+
+        ident = keep.tile([P, P], F32, name="ident", tag="q_bf", align_bytes=64)
+        make_identity(nc, ident[:])
 
         for c, width in enumerate(MM_WIDTHS):
             first = sum(MM_WIDTHS[:c])

from contextlib import ExitStack

import concourse.mybir as mybir
from concourse.masks import make_identity

D, T, I, Q = 512, 1024, 512, 128
FLOPS = 2 * D * T * Q

F32 = mybir.dt.float32
BF16 = mybir.dt.bfloat16
U32 = mybir.dt.uint32
I32 = mybir.dt.int32
U16 = mybir.dt.uint16
U8 = mybir.dt.uint8
FP8X4 = mybir.dt.float8_e4m3fn_x4
ALU = mybir.AluOpType
COPY = mybir.ActivationFunctionType.Copy

P = 128
PACK = 4
GROUP = 16
MM_WIDTHS = (256, 256, 256, 128, 128)
HALF = I // 2
N_OUT = 256
BANK = 512


def tile_attend_difference_lean_largerput_heads_kernel(
    tc, query, keys_words, keys_scales, old, offs, offs2, offs3, out
):
    nc = tc.nc
    with ExitStack() as ctx:
        keep = ctx.enter_context(tc.tile_pool(name="keep", bufs=1))
        psum = ctx.enter_context(tc.psum_pool(name="psum", bufs=1))

        list1 = keep.tile([P, I // GROUP], U16, name="list1")
        list2 = keep.tile([P, I // GROUP], U16, name="list2")
        list3 = keep.tile([P, I // GROUP], U16, name="list3")
        q_raw = keep.tile([P, PACK, Q], F32, name="q_raw")
        k_words = [
            keep.tile([P, BANK], U32, name="k_words%d" % b, align_bytes=64) for b in range(2)
        ]
        k_scales = keep.tile([P, T], U8, name="k_scales", align_bytes=64)
        old_sb = keep.tile([P, T], F32, name="old_sb")
        placed = keep.tile([P, T], F32, name="placed")
        scores = keep.tile([P, T], F32, name="scores")

        nc.vector.memset(k_scales[:].bitcast(I32), 0)
        nc.sync.dma_start(out=q_raw[:], in_=query.rearrange("(p j) q -> p j q", j=PACK))

        def load_words(b):
            nc.sync.dma_start(
                out=k_words[b][:].bitcast(I32),
                in_=keys_words[0, :, b * BANK : (b + 1) * BANK, :]
                .rearrange("p t r -> p (t r)")
                .bitcast(I32),
            )

        load_words(0)
        for quad in range(4):
            nc.sync.dma_start(
                out=k_scales[32 * quad : 32 * quad + 4, :].bitcast(I32),
                in_=keys_scales[0, 4 * quad : 4 * quad + 4, :].bitcast(I32),
            )
        load_words(1)
        nc.sync.dma_start(list1[:], offs)
        nc.sync.dma_start(list2[:], offs2)
        nc.sync.dma_start(list3[:], offs3)
        nc.sync.dma_start(out=old_sb[:], in_=old)
        nc.vector.memset(placed[:], 0.0)

        q_bf = keep.tile([P, Q, PACK], BF16, name="q_bf", tag="q_bf", align_bytes=64)
        q_words = keep.tile([P, Q], U32, name="q_words", align_bytes=64)
        q_scales = keep.tile([P, Q], U8, name="q_scales", align_bytes=64)
        halves = [slice(0, Q // 2), slice(Q // 2, Q)]
        for rows in halves:
            nc.vector.tensor_copy(
                out=q_bf[:, rows, :].rearrange("p (c i) j -> p c j i", i=4),
                in_=q_raw[:, :, rows].rearrange("p j (c i) -> p c j i", i=4),
            )
        for rows in halves:
            nc.vector.quantize_mx(
                out=q_words[:, rows].bitcast(FP8X4),
                scales=q_scales[:, rows],
                in_=q_bf[:, rows, :].rearrange("p q j -> p (q j)"),
            )

        ident = keep.tile([P, P], F32, name="ident", tag="q_bf", align_bytes=64)
        make_identity(nc, ident[:])

        for c, width in enumerate(MM_WIDTHS):
            first = sum(MM_WIDTHS[:c])
            cols = slice(first, first + width)
            bank = psum.tile([P, width], F32, name="bank%d" % c, tag="bank%d" % c)
            nc.tensor.matmul_mx(
                out=bank[:],
                lhsT=q_words[:].bitcast(FP8X4),
                lhsT_scale=q_scales[:],
                rhs=k_words[first // BANK][:, first % BANK : first % BANK + width].bitcast(FP8X4),
                rhs_scale=k_scales[:, cols],
                start=True,
                stop=True,
            )
            if c % 2 == 0:
                nc.scalar.copy(out=scores[:, cols], in_=bank[:])
            else:
                nc.vector.tensor_copy(out=scores[:, cols], in_=bank[:])

        for h in range(2):
            part = slice(h * HALF // GROUP, (h + 1) * HALF // GROUP)
            plus = keep.tile([P, HALF], F32, name="plus%d" % h)
            minus = keep.tile([P, HALF], F32, name="minus%d" % h)
            nc.scalar.activation(plus[:], scores[:].indirect(list1[:, part]), COPY)
            if h == 0:
                nc.vector.tensor_scalar(
                    minus[:], scores[:].indirect(list2[:, part]), -1.0, 0.0, ALU.mult, ALU.add
                )
            else:
                nc.scalar.activation(
                    minus[:], scores[:].indirect(list2[:, part]), COPY, scale=-1.0
                )
            nc.vector.tensor_tensor(
                placed[:].indirect(list3[:, part]), plus[:], minus[:], ALU.add
            )

        old_ps = []
        for b, factor in enumerate((1.0, 1.25)):
            turned_ps = psum.tile([P, BANK], F32, name="turned_ps%d" % b, tag="bank%d" % b)
            turned = keep.tile([P, BANK], F32, name="turned%d" % b)
            back = psum.tile([P, BANK], F32, name="back%d" % b)
            for s in range(BANK // P):
                nc.tensor.transpose(
                    turned_ps[:, s * P : (s + 1) * P],
                    old_sb[:, b * BANK + s * P : b * BANK + (s + 1) * P],
                    ident[:],
                )
            nc.scalar.activation(turned[:], turned_ps[:], COPY, scale=factor)
            for s in range(BANK // P):
                nc.tensor.transpose(
                    back[:, s * P : (s + 1) * P], turned[:, s * P : (s + 1) * P], ident[:]
                )
            old_ps.append(back)

        low = [slice(0, 256), slice(256, 512)]
        high = [slice(0, 320), slice(320, 512)]
        larger = [keep.tile([P, s.stop - s.start], F32, name="larger%d" % s.start) for s in low]
        excess = [keep.tile([P, s.stop - s.start], F32, name="excess%d" % s.start) for s in high]
        for c, part in enumerate(high):
            cols = slice(BANK + part.start, BANK + part.stop)
            nc.gpsimd.tensor_tensor(excess[c][:], placed[:, cols], old_sb[:, cols], ALU.subtract)
        for c, part in enumerate(low):
            nc.vector.tensor_tensor(larger[c][:], placed[:, part], old_ps[0][:, part], ALU.max)
        for c, part in enumerate(low):
            result = keep.tile([P, part.stop - part.start], F32, name="result_low%d" % c)
            nc.vector.scalar_tensor_tensor(
                result[:], old_ps[0][:, part], 0.25, larger[c][:], ALU.mult, ALU.add
            )
            queue = nc.sync if c % 2 == 0 else nc.scalar
            queue.dma_start(out=out[:, part], in_=result[:])
        for c, part in enumerate(high):
            cols = slice(BANK + part.start, BANK + part.stop)
            result = keep.tile([P, part.stop - part.start], F32, name="result_high%d" % c)
            nc.vector.scalar_tensor_tensor(
                result[:], excess[c][:], 0.0, old_ps[1][:, part], ALU.max, ALU.add
            )
            queue = nc.sync if c % 2 == 0 else nc.scalar
            queue.dma_start(out=out[:, cols], in_=result[:])
